import numpy as np, ml_dtypes
CORES = [4,20,60,84,92,100,116]
N = 7
import mx_ref
KT = 1
BF = ml_dtypes.bfloat16
def setup_inputs(rng):
    def f(*shape):
        return mx_ref.flush((rng.standard_normal(shape, dtype=np.float32) * np.exp2(rng.integers(-2, 3, shape[:-1] + (1,)))).astype(BF))
    return {"x": f(N, 128, KT * 512)}
def setup_inputs_blocks(rng):
    d = setup_inputs(rng)
    for k in ("x",): d[k] = mx_ref.spread(d[k], rng, 4)
    return d
def setup_inputs_wide(rng):
    d = setup_inputs(rng)
    for k in ("x",): d[k] = mx_ref.flush((d[k].astype(np.float32) * np.exp2(rng.integers(-8, 9, (N, 1, 1))).astype(np.float32)).astype(BF))
    return d
def setup_inputs_zeros(rng):
    d = setup_inputs(rng); v = d["x"].reshape(N, 128, -1, 4).copy()
    v[np.broadcast_to((rng.random((N, 1, v.shape[2], 1)) < 0.33), v.shape)] = 0
    d["x"] = v.reshape(d["x"].shape)
    return d
def reference(x):
    Q = [[mx_ref.quantize(x[j][:, 512 * t:512 * t + 512]) for t in range(KT)] for j in range(N)]
    y = np.zeros((N, 128, N * 128), np.float32)
    for r in range(N):
        for j in range(N):
            for t in range(KT):
                p = mx_ref.matmul(Q[r][t], Q[j][t])
                y[r][:, 128 * j:128 * j + 128] = p if t == 0 else y[r][:, 128 * j:128 * j + 128] + p
    return {"y": y}

@@ -1,0 +1,139 @@
+from concourse.bass import DstId, RemoteDMATransfer
+from concourse.mybir import dt, ActivationFunctionType
+
+N = 7
+W = 128
+BANK = 512
+
+MAX_HELPERS = 3
+HOP_COST = 2.0
+
+SCRATCH = {
+    "xt": ("sbuf", [128, 4 * W], "bfloat16"),
+    "q": ("sbuf", [128, N * W], "float8_e4m3fn_x4"),
+    "s": ("sbuf", [128, N * W], "uint8"),
+    "acc": ("psum", [128, N * BANK], "float32"),
+    "o": ("sbuf", [128, N * W], "float32"),
+}
+SEMAPHORES = (["ld", "qd", "sent", "st"] + ["as%d" % j for j in range(N)] + ["ac%d" % j for j in range(N)]
+              + ["mm%d" % j for j in range(N)] + ["cp%d" % j for j in range(N)])
+
+
+def _bits(mask):
+    return bin(mask).count("1")
+
+
+def _plan(cores, topo):
+    n = len(cores)
+    every = range(topo.CHIPS * topo.CORES_PER_CHIP)
+    send, helper, eta = [], {}, [[] for _ in cores]
+    for i, c in enumerate(cores):
+        others = [(i + k) % n for k in range(1, n)]
+        near = [j for j in others if topo.may_write(c, cores[j])]
+        far = [j for j in others if not topo.may_write(c, cores[j])]
+        turn = i % max(1, len(far))
+        far = far[turn:] + far[:turn]
+        cands = [h for h in every if topo.chip(h) == topo.chip(c) and h not in cores
+                 and all(topo.may_write(h, cores[j]) for j in far)]
+        cands.sort(key=lambda h: (topo.die(h) != topo.die(c), h))
+        hs = cands[:min(MAX_HELPERS, len(far))]
+        lists = [far[k::len(hs)] for k in range(len(hs))] if hs else []
+        lo = ~0
+        for j in near:
+            lo &= topo.mask(c, cores[j])
+        hi = 0
+        for h in hs:
+            hi |= topo.mask(c, h)
+        if not near:
+            lo = hi
+        hi &= ~lo
+        groups = [[lo, [], list(near)], [hi, [], []]]
+        for k, h in enumerate(hs):
+            load = [len(gr[1]) + len(gr[2]) for gr in groups]
+            pick = 1 if (hi and load[1] < load[0]) else 0
+            groups[pick][1].append(k)
+        calls = []
+        for mask, hk, rk in groups:
+            if not (hk or rk):
+                continue
+            calls.append((mask, [hs[k] for k in hk] + [cores[j] for j in rk]))
+            for pos, k in enumerate(hk):
+                m2 = ~0
+                for j in lists[k]:
+                    m2 &= topo.mask(hs[k], cores[j])
+                helper[hs[k]] = (i, _bits(mask), m2, [cores[j] for j in lists[k]])
+                for p2, j in enumerate(lists[k]):
+                    eta[j].append((pos + 1 + HOP_COST + p2 + 1, (j - i) % n, i, _bits(m2)))
+            for pos, j in enumerate(rk):
+                eta[j].append((len(hk) + pos + 1, (j - i) % n, i, _bits(mask)))
+        send.append(calls)
+    arrive = [[(i, e) for _, _, i, e in sorted(lst)] for lst in eta]
+    return send, helper, arrive
+
+
+def _views(T, j):
+    cols = slice(j * W, (j + 1) * W)
+    return ((T.s[:, cols], T.sem["as%d" % j]), (T.q[:, cols].bitcast(dt.uint8), T.sem["ac%d" % j]))
+
+
+def _fused(g, T, topo, view, sem, calls):
+    trs = []
+    for mask, dests in calls:
+        ids = []
+        for d in dests:
+            rid, pid, _ = topo.addr(d)
+            ids.append(DstId(rid=rid, pnc=pid))
+        trs.append(RemoteDMATransfer(dst_ids=ids, dma_engine_mask=mask, remote_sem=sem,
+                                     srcs=[view], dsts=[view for _ in dests]))
+    g.remote_dma_fused(trs, local_sem=T.sem.sent)
+    return sum(_bits(mask) for mask, _ in calls)
+
+
+def rank_program(g, core, T, topo):
+    send, helper, arrive = _plan(list(T.cores), topo)
+    rank = T.rank_of(core)
+
+    if rank is None:
+        if core not in helper:
+            return
+        src, n_in, mask, dests = helper[core]
+        left = 0
+        for view, sem in _views(T, src):
+            g.wait_ge(sem, n_in)
+            left += _fused(g, T, topo, view, sem, [(mask, dests)])
+        g.wait_ge(T.sem.sent, left)
+        return
+
+    own = slice(rank * W, (rank + 1) * W)
+    g.sync.dma_start(T.xt[:], T.x[:]).then_inc(T.sem.ld, 16)
+    g.vector.wait_ge(T.sem.ld, 16)
+    g.vector.quantize_mx(T.q[:, own], T.s[:, own], T.xt[:]).then_inc(T.sem.qd, 1)
+
+    g.wait_ge(T.sem.qd, 1)
+    left = 0
+    for view, sem in _views(T, rank):
+        left += _fused(g, T, topo, view, sem, send[rank])
+
+    g.tensor.wait_ge(T.sem.qd, 1)
+    order = [(rank, 0)] + arrive[rank]
+    for k, (j, n_in) in enumerate(order):
+        cols = slice(j * W, (j + 1) * W)
+        bank = T.acc[:, j * BANK:j * BANK + W]
+        mm, cp = T.sem["mm%d" % j], T.sem["cp%d" % j]
+        if j != rank:
+            g.tensor.wait_ge(T.sem["as%d" % j], n_in)
+            g.tensor.wait_ge(T.sem["ac%d" % j], n_in)
+        g.tensor.matmul_mx(bank, T.q[:, own], T.s[:, own], T.q[:, cols], T.s[:, cols], True, True).then_inc(mm, 1)
+        if k % 2 == 0:
+            g.vector.wait_ge(mm, 1)
+            g.vector.tensor_copy(T.o[:, cols], bank).then_inc(cp, 1)
+            dq = g.sync
+        else:
+            g.scalar.wait_ge(mm, 1)
+            g.scalar.activation(T.o[:, cols], bank, ActivationFunctionType.Copy).then_inc(cp, 1)
+            dq = g.scalar
+        dq.wait_ge(cp, 1)
+        dq.dma_start(T.y[:, cols], T.o[:, cols]).then_inc(T.sem.st, 16)
+
+    g.wait_ge(T.sem.sent, left)
+    g.wait_ge(T.sem.st, 16 * len(order))

@@ -5,8 +5,8 @@ N = 7
 W = 128
 BANK = 512
 
-MAX_HELPERS = 3
-HOP_COST = 2.0
+MAX_DIRECT = 3
+HOP_COST = 3.0
 
 SCRATCH = {
     "xt": ("sbuf", [128, 4 * W], "bfloat16"),
@@ -26,47 +26,47 @@ def _bits(mask):
 def _plan(cores, topo):
     n = len(cores)
     every = range(topo.CHIPS * topo.CORES_PER_CHIP)
+    intake = [{} for _ in cores]
+    direct, lists = [], [{} for _ in cores]
+    for i, c in enumerate(cores):
+        near = [(i + k) % n for k in range(1, n) if topo.may_write(c, cores[(i + k) % n])]
+        direct.append(near[:MAX_DIRECT])
+        for j in direct[i]:
+            intake[j][topo.die(c)] = intake[j].get(topo.die(c), 0) + 1
+    for k in range(1, n):
+        for i, c in enumerate(cores):
+            j = (i + k) % n
+            if j in direct[i]:
+                continue
+            cands = [h for h in every if topo.chip(h) == topo.chip(c) and h not in cores
+                     and topo.may_write(h, cores[j])]
+            best = min(cands, key=lambda h: (len(lists[i].get(h, [])), intake[j].get(topo.die(h), 0),
+                                             sum(topo.may_write(h, d) for d in cores),
+                                             topo.die(h) != topo.die(c), h))
+            lists[i].setdefault(best, []).append(j)
+            intake[j][topo.die(best)] = intake[j].get(topo.die(best), 0) + 1
+
     send, helper, eta = [], {}, [[] for _ in cores]
     for i, c in enumerate(cores):
-        others = [(i + k) % n for k in range(1, n)]
-        near = [j for j in others if topo.may_write(c, cores[j])]
-        far = [j for j in others if not topo.may_write(c, cores[j])]
-        turn = i % max(1, len(far))
-        far = far[turn:] + far[:turn]
-        cands = [h for h in every if topo.chip(h) == topo.chip(c) and h not in cores
-                 and all(topo.may_write(h, cores[j]) for j in far)]
-        cands.sort(key=lambda h: (topo.die(h) != topo.die(c), h))
-        hs = cands[:min(MAX_HELPERS, len(far))]
-        lists = [far[k::len(hs)] for k in range(len(hs))] if hs else []
+        hs = sorted(lists[i], key=lambda h: (-len(lists[i][h]), topo.die(h) != topo.die(c), h))
         lo = ~0
-        for j in near:
+        for j in direct[i]:
             lo &= topo.mask(c, cores[j])
-        hi = 0
+        hi = ~0
         for h in hs:
-            hi |= topo.mask(c, h)
-        if not near:
-            lo = hi
-        hi &= ~lo
-        groups = [[lo, [], list(near)], [hi, [], []]]
-        for k, h in enumerate(hs):
-            load = [len(gr[1]) + len(gr[2]) for gr in groups]
-            pick = 1 if (hi and load[1] < load[0]) else 0
-            groups[pick][1].append(k)
-        calls = []
-        for mask, hk, rk in groups:
-            if not (hk or rk):
-                continue
-            calls.append((mask, [hs[k] for k in hk] + [cores[j] for j in rk]))
-            for pos, k in enumerate(hk):
-                m2 = ~0
-                for j in lists[k]:
-                    m2 &= topo.mask(hs[k], cores[j])
-                helper[hs[k]] = (i, _bits(mask), m2, [cores[j] for j in lists[k]])
-                for p2, j in enumerate(lists[k]):
-                    eta[j].append((pos + 1 + HOP_COST + p2 + 1, (j - i) % n, i, _bits(m2)))
-            for pos, j in enumerate(rk):
-                eta[j].append((len(hk) + pos + 1, (j - i) % n, i, _bits(mask)))
-        send.append(calls)
+            hi &= topo.mask(c, h)
+        if direct[i] and (hi & ~lo):
+            hi &= ~lo
+        send.append(((hi, hs), (lo, [cores[j] for j in direct[i]])))
+        for pos, h in enumerate(hs):
+            m2 = ~0
+            for j in lists[i][h]:
+                m2 &= topo.mask(h, cores[j])
+            helper[h] = (i, _bits(hi), m2, [cores[j] for j in lists[i][h]])
+            for p2, j in enumerate(lists[i][h]):
+                eta[j].append((pos + 1 + HOP_COST + p2 + 1, (j - i) % n, i, _bits(m2)))
+        for pos, j in enumerate(direct[i]):
+            eta[j].append((pos + 1, (j - i) % n, i, _bits(lo)))
     arrive = [[(i, e) for _, _, i, e in sorted(lst)] for lst in eta]
     return send, helper, arrive
 
@@ -76,17 +76,16 @@ def _views(T, j):
     return ((T.s[:, cols], T.sem["as%d" % j]), (T.q[:, cols].bitcast(dt.uint8), T.sem["ac%d" % j]))
 
 
-def _fused(g, T, topo, view, sem, calls):
-    trs = []
-    for mask, dests in calls:
-        ids = []
-        for d in dests:
-            rid, pid, _ = topo.addr(d)
-            ids.append(DstId(rid=rid, pnc=pid))
-        trs.append(RemoteDMATransfer(dst_ids=ids, dma_engine_mask=mask, remote_sem=sem,
-                                     srcs=[view], dsts=[view for _ in dests]))
-    g.remote_dma_fused(trs, local_sem=T.sem.sent)
-    return sum(_bits(mask) for mask, _ in calls)
+def _write(g, T, topo, view, sem, mask, dests):
+    if not dests:
+        return 0
+    ids = []
+    for d in dests:
+        rid, pid, _ = topo.addr(d)
+        ids.append(DstId(rid=rid, pnc=pid))
+    g.remote_dma_fused([RemoteDMATransfer(dst_ids=ids, dma_engine_mask=mask, remote_sem=sem,
+                                          srcs=[view], dsts=[view for _ in dests])], local_sem=T.sem.sent)
+    return _bits(mask)
 
 
 def rank_program(g, core, T, topo):
@@ -100,7 +99,7 @@ def rank_program(g, core, T, topo):
         left = 0
         for view, sem in _views(T, src):
             g.wait_ge(sem, n_in)
-            left += _fused(g, T, topo, view, sem, [(mask, dests)])
+            left += _write(g, T, topo, view, sem, mask, dests)
         g.wait_ge(T.sem.sent, left)
         return
 
@@ -111,8 +110,9 @@ def rank_program(g, core, T, topo):
 
     g.wait_ge(T.sem.qd, 1)
     left = 0
-    for view, sem in _views(T, rank):
-        left += _fused(g, T, topo, view, sem, send[rank])
+    for mask, dests in send[rank]:
+        for view, sem in _views(T, rank):
+            left += _write(g, T, topo, view, sem, mask, dests)
 
     g.tensor.wait_ge(T.sem.qd, 1)
     order = [(rank, 0)] + arrive[rank]

from concourse.bass import DstId, RemoteDMATransfer
from concourse.mybir import dt, ActivationFunctionType

N = 7
W = 128
BANK = 512

MAX_DIRECT = 3
HOP_COST = 3.0

SCRATCH = {
    "xt": ("sbuf", [128, 4 * W], "bfloat16"),
    "q": ("sbuf", [128, N * W], "float8_e4m3fn_x4"),
    "s": ("sbuf", [128, N * W], "uint8"),
    "acc": ("psum", [128, N * BANK], "float32"),
    "o": ("sbuf", [128, N * W], "float32"),
}
SEMAPHORES = (["ld", "qd", "sent", "st"] + ["as%d" % j for j in range(N)] + ["ac%d" % j for j in range(N)]
              + ["mm%d" % j for j in range(N)] + ["cp%d" % j for j in range(N)])


def _bits(mask):
    return bin(mask).count("1")


def _plan(cores, topo):
    n = len(cores)
    every = range(topo.CHIPS * topo.CORES_PER_CHIP)
    intake = [{} for _ in cores]
    direct, lists = [], [{} for _ in cores]
    for i, c in enumerate(cores):
        near = [(i + k) % n for k in range(1, n) if topo.may_write(c, cores[(i + k) % n])]
        direct.append(near[:MAX_DIRECT])
        for j in direct[i]:
            intake[j][topo.die(c)] = intake[j].get(topo.die(c), 0) + 1
    for k in range(1, n):
        for i, c in enumerate(cores):
            j = (i + k) % n
            if j in direct[i]:
                continue
            cands = [h for h in every if topo.chip(h) == topo.chip(c) and h not in cores
                     and topo.may_write(h, cores[j])]
            best = min(cands, key=lambda h: (len(lists[i].get(h, [])), intake[j].get(topo.die(h), 0),
                                             sum(topo.may_write(h, d) for d in cores),
                                             topo.die(h) != topo.die(c), h))
            lists[i].setdefault(best, []).append(j)
            intake[j][topo.die(best)] = intake[j].get(topo.die(best), 0) + 1

    send, helper, eta = [], {}, [[] for _ in cores]
    for i, c in enumerate(cores):
        hs = sorted(lists[i], key=lambda h: (-len(lists[i][h]), topo.die(h) != topo.die(c), h))
        lo = ~0
        for j in direct[i]:
            lo &= topo.mask(c, cores[j])
        hi = ~0
        for h in hs:
            hi &= topo.mask(c, h)
        if direct[i] and (hi & ~lo):
            hi &= ~lo
        send.append(((hi, hs), (lo, [cores[j] for j in direct[i]])))
        for pos, h in enumerate(hs):
            m2 = ~0
            for j in lists[i][h]:
                m2 &= topo.mask(h, cores[j])
            helper[h] = (i, _bits(hi), m2, [cores[j] for j in lists[i][h]])
            for p2, j in enumerate(lists[i][h]):
                eta[j].append((pos + 1 + HOP_COST + p2 + 1, (j - i) % n, i, _bits(m2)))
        for pos, j in enumerate(direct[i]):
            eta[j].append((pos + 1, (j - i) % n, i, _bits(lo)))
    arrive = [[(i, e) for _, _, i, e in sorted(lst)] for lst in eta]
    return send, helper, arrive


def _views(T, j):
    cols = slice(j * W, (j + 1) * W)
    return ((T.s[:, cols], T.sem["as%d" % j]), (T.q[:, cols].bitcast(dt.uint8), T.sem["ac%d" % j]))


def _write(g, T, topo, view, sem, mask, dests):
    if not dests:
        return 0
    ids = []
    for d in dests:
        rid, pid, _ = topo.addr(d)
        ids.append(DstId(rid=rid, pnc=pid))
    g.remote_dma_fused([RemoteDMATransfer(dst_ids=ids, dma_engine_mask=mask, remote_sem=sem,
                                          srcs=[view], dsts=[view for _ in dests])], local_sem=T.sem.sent)
    return _bits(mask)


def rank_program(g, core, T, topo):
    send, helper, arrive = _plan(list(T.cores), topo)
    rank = T.rank_of(core)

    if rank is None:
        if core not in helper:
            return
        src, n_in, mask, dests = helper[core]
        left = 0
        for view, sem in _views(T, src):
            g.wait_ge(sem, n_in)
            left += _write(g, T, topo, view, sem, mask, dests)
        g.wait_ge(T.sem.sent, left)
        return

    own = slice(rank * W, (rank + 1) * W)
    g.sync.dma_start(T.xt[:], T.x[:]).then_inc(T.sem.ld, 16)
    g.vector.wait_ge(T.sem.ld, 16)
    g.vector.quantize_mx(T.q[:, own], T.s[:, own], T.xt[:]).then_inc(T.sem.qd, 1)

    g.wait_ge(T.sem.qd, 1)
    left = 0
    for mask, dests in send[rank]:
        for view, sem in _views(T, rank):
            left += _write(g, T, topo, view, sem, mask, dests)

    g.tensor.wait_ge(T.sem.qd, 1)
    order = [(rank, 0)] + arrive[rank]
    for k, (j, n_in) in enumerate(order):
        cols = slice(j * W, (j + 1) * W)
        bank = T.acc[:, j * BANK:j * BANK + W]
        mm, cp = T.sem["mm%d" % j], T.sem["cp%d" % j]
        if j != rank:
            g.tensor.wait_ge(T.sem["as%d" % j], n_in)
            g.tensor.wait_ge(T.sem["ac%d" % j], n_in)
        g.tensor.matmul_mx(bank, T.q[:, own], T.s[:, own], T.q[:, cols], T.s[:, cols], True, True).then_inc(mm, 1)
        if k % 2 == 0:
            g.vector.wait_ge(mm, 1)
            g.vector.tensor_copy(T.o[:, cols], bank).then_inc(cp, 1)
            dq = g.sync
        else:
            g.scalar.wait_ge(mm, 1)
            g.scalar.activation(T.o[:, cols], bank, ActivationFunctionType.Copy).then_inc(cp, 1)
            dq = g.scalar
        dq.wait_ge(cp, 1)
        dq.dma_start(T.y[:, cols], T.o[:, cols]).then_inc(T.sem.st, 16)

    g.wait_ge(T.sem.sent, left)
    g.wait_ge(T.sem.st, 16 * len(order))
